import numpy as np
import ml_dtypes


def mxq(x, axis, fmt="e4m3"):
    dtype, down = {"e4m3": (ml_dtypes.float8_e4m3fn, 7), "e5m2": (ml_dtypes.float8_e5m2, 14)}[fmt]
    v = np.moveaxis(np.asarray(x, np.float32).astype(ml_dtypes.bfloat16).astype(np.float64), axis, -1)
    blocks = v.reshape(v.shape[:-1] + (-1, 32))
    amax = np.abs(blocks).max(-1, keepdims=True)
    byte = np.maximum(np.where(amax > 0, np.frexp(amax)[1] - 1 + 127, 0) - down, 1)
    scale = np.exp2(byte - 127.0)
    codes = (blocks / scale).astype(np.float32).astype(dtype).astype(np.float64)
    return np.moveaxis((codes * scale).reshape(v.shape), -1, axis)


WIDE = False


def mx_kscale(k):
    if not WIDE:
        return np.ones(k)
    levels = np.array([10, -10, 5, -5, 0])
    if k % 512:
        return np.exp2(np.random.permutation(np.resize(levels, k // 32))).repeat(32)
    a = np.empty((k // 512, 16))
    for p in range(k // 512):
        a[p, :8] = np.random.permutation(np.resize(levels, 8))
        for g in range(8):
            far = levels[np.abs(levels - a[p, g]) >= 10]
            a[p, g + 8] = far[np.random.randint(len(far))]
    return np.exp2(a.ravel()).repeat(32)


def f64(x):
    return np.asarray(x).astype(np.float64)


def striped(idx):
    return np.tile(idx.reshape(-1, 16).T, (8, 1)).astype(np.uint16)


def unstriped(offs):
    return offs[:16].T.reshape(-1).astype(np.int64)


def pack_weight(w):
    k, n = w.shape
    w = f64(np.asarray(w, np.float32).astype(ml_dtypes.bfloat16)).reshape(k // 32, 32, n)
    amax = np.abs(w).max(1)
    byte = np.clip(np.where(amax > 0, np.frexp(amax)[1] - 1 + 127 - 7, 1), 1, 254)
    scaled = (w * np.exp2(127.0 - byte)[:, None, :]).reshape(k, n).astype(np.float32)
    words = np.ascontiguousarray(scaled.reshape(k // 512, 128, 4, n).transpose(0, 1, 3, 2)).astype(ml_dtypes.float8_e4m3fn).view(np.uint8)
    return words, np.ascontiguousarray(byte.astype(np.uint8).reshape(k // 512, 16, n))


def unpack_weight(words, scales):
    g, p, n, _ = words.shape
    vals = np.ascontiguousarray(words).view(ml_dtypes.float8_e4m3fn).astype(np.float64) * np.repeat(np.exp2(scales.astype(np.float64) - 127.0), 8, axis=1)[..., None]
    return vals.transpose(0, 1, 3, 2).reshape(g * 512, n)


def sigmoid(v):
    return 1.0 / (1.0 + np.exp(-np.maximum(v, -700.0)))


K, T, S, D, N, W = 512, 1024, 512, 4, 256, 1024
P = 2 ** 7


def setup_inputs():
    n = np.random.standard_normal
    s = mx_kscale(K)[:, None]
    packed_xT = pack_weight(n((K, T)) * s)
    packed_eT = pack_weight(n((K, W)) * s)
    return {
        "x_words": packed_xT[0],
        "x_scales": packed_xT[1],
        "e_words": packed_eT[0],
        "e_scales": packed_eT[1],
        "w1": (n((K, N)) / np.sqrt(K) / s).astype(np.float32),
        "w2": (n((K, N)) / np.sqrt(K) / s).astype(np.float32),
        "click": (np.tile((np.random.uniform(size=S) < 0.3) * 1.0, (P, 1))).astype(np.float32),
        "offs": striped(np.random.permutation(T)[:S]),
        "cxt": striped(np.random.permutation(W)[:S]),
    }


def reference(x_words, x_scales, e_words, e_scales, w1, w2, click, offs, cxt):
    e_cxt = unpack_weight(e_words, e_scales)[:, unstriped(cxt)]
    exa = sigmoid(mxq(f64(w2), 0, "e4m3").T @ e_cxt)
    xq = unpack_weight(x_words, x_scales)[:, unstriped(offs)]
    rel = sigmoid(mxq(f64(w1), 0, "e4m3").T @ xq)
    den = -0.98 * (rel * exa) + 1.0
    qq = (exa - (rel * exa)) / den
    post = f64(click)[:1] + qq - (f64(click)[:1] * qq)
    return post.reshape(len(post), -1, D).mean(axis=2)

@@ -1,0 +1,168 @@
+import math
+from contextlib import ExitStack
+
+import concourse.mybir as mybir
+from concourse.masks import make_identity
+
+F32 = mybir.dt.float32
+BF16 = mybir.dt.bfloat16
+I32 = mybir.dt.int32
+U32 = mybir.dt.uint32
+U16 = mybir.dt.uint16
+U8 = mybir.dt.uint8
+FP8X4 = mybir.dt.float8_e4m3fn_x4
+ACT = mybir.ActivationFunctionType
+ALU = mybir.AluOpType
+
+P = 128
+PACK = 4
+K, T, S, D, N = 512, 1024, 512, 4, 256
+M_TILES = N // P
+CHUNKS = 2
+J = S // CHUNKS
+V = J // D
+KEEP = 0.98
+REST = 1.0 - KEEP
+FLOPS = 2 * 2 * K * N * S
+
+
+def tile_picked_ytrust_exam_p_kernel(
+    tc, x_words, x_scales, e_words, e_scales, w1, w2, click, offs, cxt, out
+):
+    nc = tc.nc
+    with ExitStack() as ctx:
+        sb = ctx.enter_context(tc.tile_pool(name="sb", bufs=1))
+        ps = ctx.enter_context(tc.psum_pool(name="ps", bufs=1))
+
+        offs_sb = sb.tile([P, S // 16], U16, name="offs_sb")
+        cxt_sb = sb.tile([P, S // 16], U16, name="cxt_sb")
+        x_tab = sb.tile([P, T], U32, name="x_tab", align_bytes=64)
+        e_tab = sb.tile([P, T], U32, name="e_tab", align_bytes=64)
+        x_stab = sb.tile([P, T], U8, name="x_stab", align_bytes=64)
+        e_stab = sb.tile([P, T], U8, name="e_stab", tag="e_stab_then_w1_scales", align_bytes=64)
+        w1_raw = sb.tile([P, PACK, N], F32, name="w1_raw", align_bytes=64)
+        w2_raw = sb.tile([P, PACK, N], F32, name="w2_raw", align_bytes=64)
+        click_col = sb.tile([P, D], F32, name="click_col", align_bytes=64)
+        ident = sb.tile([P, P], F32, name="ident", align_bytes=64)
+
+        def load_words(tab, words):
+            nc.sync.dma_start(out=tab[:].bitcast(I32), in_=words[0].rearrange("p n t -> p (n t)").bitcast(I32))
+
+        def load_scales(stab, scales):
+            for q in range(4):
+                nc.sync.dma_start(
+                    out=stab[32 * q : 32 * q + 4, :].bitcast(I32),
+                    in_=scales[0, 4 * q : 4 * q + 4, :].bitcast(I32),
+                )
+
+        def load_weight(raw, w):
+            nc.sync.dma_start(out=raw[:], in_=w.rearrange("(p t) m -> p t m", t=PACK))
+
+        nc.vector.memset(x_stab[:].bitcast(I32), 0)
+        nc.vector.memset(e_stab[:].bitcast(I32), 0)
+        nc.sync.dma_start(offs_sb[:], offs)
+        load_scales(x_stab, x_scales)
+        nc.sync.dma_start(cxt_sb[:], cxt)
+        load_words(x_tab, x_words)
+        load_weight(w1_raw, w1)
+        load_scales(e_stab, e_scales)
+        load_weight(w2_raw, w2)
+        load_words(e_tab, e_words)
+        nc.sync.dma_start(out=click_col[:], in_=click[0].rearrange("(v d) -> v d", d=D))
+        make_identity(nc, ident[:])
+
+        def interleave(raw, name):
+            grouped = sb.tile([P, N, PACK], BF16, name=name, align_bytes=64)
+            nc.scalar.copy(out=grouped[:], in_=raw[:].rearrange("p t m -> p m t"))
+            return grouped
+
+        def quantize(grouped, name, tag):
+            codes = sb.tile([P, N], U32, name=name + "_codes", align_bytes=64)
+            scales = sb.tile([P, N], U8, name=name + "_scales", tag=tag, align_bytes=64)
+            nc.vector.quantize_mx(
+                out=codes[:].bitcast(FP8X4), scales=scales[:], in_=grouped[:].rearrange("p m t -> p (m t)")
+            )
+            return codes, scales
+
+        def gather(tab, lst, c0, n, dtype, name):
+            picked = sb.tile([P, n], dtype, name=name, align_bytes=64)
+            nc.vector.tensor_copy(picked[:], tab[:].indirect(lst[:, c0 // 16 : (c0 + n) // 16]))
+            return picked
+
+        def product(wq, codes, scales, name):
+            bank = ps.tile([P, M_TILES, J], F32, name=name)
+            for m in range(M_TILES):
+                nc.tensor.matmul_mx(
+                    out=bank[:, m, :],
+                    lhsT=wq[0][:, m * P : (m + 1) * P].bitcast(FP8X4),
+                    lhsT_scale=wq[1][:, m * P : (m + 1) * P],
+                    rhs=codes.bitcast(FP8X4),
+                    rhs_scale=scales,
+                    start=True,
+                    stop=True,
+                )
+            return bank
+
+        def sigmoid(bank, scale, bias, name):
+            res = sb.tile([P, D, M_TILES, V], F32, name=name, align_bytes=64)
+            nc.scalar.activation(
+                out=res[:], in_=bank[:].rearrange("p m (v d) -> p d m v", d=D), func=ACT.Sigmoid, scale=scale, bias=bias
+            )
+            return res
+
+        w1_grp = interleave(w1_raw, "w1_grp")
+        w2_grp = interleave(w2_raw, "w2_grp")
+
+        x_sc = gather(x_stab, offs_sb, 0, S, U8, "x_sc")
+        x_codes = gather(x_tab, offs_sb, 0, S, U32, "x_codes")
+        e_sc = gather(e_stab, cxt_sb, 0, S, U8, "e_sc")
+        w1q = quantize(w1_grp, "w1", "e_stab_then_w1_scales")
+        miss = []
+        for c in range(CHUNKS):
+            bank = product(w1q, x_codes[:, c * J : (c + 1) * J], x_sc[:, c * J : (c + 1) * J], "x_bank%d" % c)
+            miss.append(sigmoid(bank, -1.0, 0.0, "miss%d" % c))
+
+        w2q = quantize(w2_grp, "w2", "w2_scales")
+        seen = []
+        for c in range(CHUNKS):
+            e_codes = gather(e_tab, cxt_sb, c * J, J, U32, "e_codes%d" % c)
+            bank = product(w2q, e_codes[:], e_sc[:, c * J : (c + 1) * J], "e_bank%d" % c)
+            seen.append(sigmoid(bank, 1.0, math.log(REST), "seen%d" % c))
+
+        click_bank = ps.tile([P, D, P], F32, name="click_bank")
+        for d in range(D):
+            nc.tensor.transpose(click_bank[:, d, :], click_col[:, d : d + 1].to_broadcast([P, P]), ident[:])
+
+        flat = "p d m v -> p (d m v)"
+        held = []
+        for c in range(CHUNKS):
+            both = sb.tile([P, D, M_TILES, V], F32, name="both%d" % c, align_bytes=64)
+            nc.vector.tensor_tensor(both[:].rearrange(flat), miss[c][:].rearrange(flat), seen[c][:].rearrange(flat), ALU.mult)
+            lifted = sb.tile([P, D, M_TILES, V], F32, name="lifted%d" % c, align_bytes=64)
+            clicks = click_bank[:, :, c * V : (c + 1) * V].unsqueeze(2).broadcast_to([P, D, M_TILES, V])
+            nc.vector.tensor_tensor(lifted[:], both[:], clicks, ALU.max)
+            held.append(lifted)
+
+        roots = []
+        for c in range(CHUNKS):
+            root = sb.tile([P, D * M_TILES * V], F32, name="root%d" % c, align_bytes=64)
+            nc.scalar.activation(
+                out=root[:], in_=held[c][:].rearrange(flat), func=ACT.Abs_reciprocal_sqrt,
+                scale=D * KEEP * KEEP / REST, bias=D * KEEP,
+            )
+            roots.append(root)
+
+        half = D * M_TILES * V // 2
+        for c in range(CHUNKS):
+            inv = sb.tile([P, 2 * half], F32, name="inv%d" % c, align_bytes=64)
+            if c == 0:
+                nc.vector.tensor_tensor(inv[:], roots[c][:], roots[c][:], ALU.mult)
+            else:
+                nc.scalar.activation(out=inv[:], in_=roots[c][:], func=ACT.Square)
+            pair = sb.tile([P, half], F32, name="pair%d" % c, align_bytes=64)
+            nc.vector.scalar_tensor_tensor(pair[:], inv[:, :half], -1.0, inv[:, half:], ALU.mult, ALU.subtract)
+            res = sb.tile([P, M_TILES, V], F32, name="res%d" % c, align_bytes=64)
+            nc.vector.scalar_tensor_tensor(
+                res[:].rearrange("p m v -> p (m v)"), pair[:, : half // 2], 1.0 / KEEP, pair[:, half // 2 :], ALU.add, ALU.add
+            )
+            nc.sync.dma_start(out=out.rearrange("(m p) v -> p m v", p=P)[:, :, c * V : (c + 1) * V], in_=res[:])

@@ -39,9 +39,9 @@ def tile_picked_ytrust_exam_p_kernel(
         x_tab = sb.tile([P, T], U32, name="x_tab", align_bytes=64)
         e_tab = sb.tile([P, T], U32, name="e_tab", align_bytes=64)
         x_stab = sb.tile([P, T], U8, name="x_stab", align_bytes=64)
-        e_stab = sb.tile([P, T], U8, name="e_stab", tag="e_stab_then_w1_scales", align_bytes=64)
+        e_stab = sb.tile([P, T], U8, name="e_stab", tag="e_stab_then_w2_scales", align_bytes=64)
         w1_raw = sb.tile([P, PACK, N], F32, name="w1_raw", align_bytes=64)
-        w2_raw = sb.tile([P, PACK, N], F32, name="w2_raw", align_bytes=64)
+        w2_raw = sb.tile([P, PACK, N], F32, name="w2_raw", tag="w2_raw_then_miss", align_bytes=64)
         click_col = sb.tile([P, D], F32, name="click_col", align_bytes=64)
         ident = sb.tile([P, P], F32, name="ident", align_bytes=64)
 
@@ -60,15 +60,18 @@ def tile_picked_ytrust_exam_p_kernel(
 
         nc.vector.memset(x_stab[:].bitcast(I32), 0)
         nc.vector.memset(e_stab[:].bitcast(I32), 0)
+        warm = sb.tile([P, 2], F32, name="warm", align_bytes=64)
+        nc.vector.memset(warm[:, 0:1], 0.0)
+        nc.scalar.activation(out=warm[:, 1:2], in_=warm[:, 0:1], func=ACT.Sigmoid)
         nc.sync.dma_start(offs_sb[:], offs)
-        load_scales(x_stab, x_scales)
-        nc.sync.dma_start(cxt_sb[:], cxt)
         load_words(x_tab, x_words)
+        load_scales(x_stab, x_scales)
         load_weight(w1_raw, w1)
-        load_scales(e_stab, e_scales)
         load_weight(w2_raw, w2)
+        nc.sync.dma_start(cxt_sb[:], cxt)
+        load_scales(e_stab, e_scales)
         load_words(e_tab, e_words)
-        nc.sync.dma_start(out=click_col[:], in_=click[0].rearrange("(v d) -> v d", d=D))
+        nc.gpsimd.dma_start(out=click_col[:], in_=click[0].rearrange("(v d) -> v d", d=D))
         make_identity(nc, ident[:])
 
         def interleave(raw, name):
@@ -90,7 +93,7 @@ def tile_picked_ytrust_exam_p_kernel(
             return picked
 
         def product(wq, codes, scales, name):
-            bank = ps.tile([P, M_TILES, J], F32, name=name)
+            bank = ps.tile([P, M_TILES, codes.shape[1]], F32, name=name)
             for m in range(M_TILES):
                 nc.tensor.matmul_mx(
                     out=bank[:, m, :],
@@ -103,66 +106,64 @@ def tile_picked_ytrust_exam_p_kernel(
                 )
             return bank
 
-        def sigmoid(bank, scale, bias, name):
-            res = sb.tile([P, D, M_TILES, V], F32, name=name, align_bytes=64)
+        def sigmoid(res, bank, scale, bias):
             nc.scalar.activation(
-                out=res[:], in_=bank[:].rearrange("p m (v d) -> p d m v", d=D), func=ACT.Sigmoid, scale=scale, bias=bias
+                out=res, in_=bank[:].rearrange("p m (v d) -> p d m v", d=D), func=ACT.Sigmoid, scale=scale, bias=bias
             )
-            return res
-
-        w1_grp = interleave(w1_raw, "w1_grp")
-        w2_grp = interleave(w2_raw, "w2_grp")
-
-        x_sc = gather(x_stab, offs_sb, 0, S, U8, "x_sc")
-        x_codes = gather(x_tab, offs_sb, 0, S, U32, "x_codes")
-        e_sc = gather(e_stab, cxt_sb, 0, S, U8, "e_sc")
-        w1q = quantize(w1_grp, "w1", "e_stab_then_w1_scales")
-        miss = []
-        for c in range(CHUNKS):
-            bank = product(w1q, x_codes[:, c * J : (c + 1) * J], x_sc[:, c * J : (c + 1) * J], "x_bank%d" % c)
-            miss.append(sigmoid(bank, -1.0, 0.0, "miss%d" % c))
-
-        w2q = quantize(w2_grp, "w2", "w2_scales")
-        seen = []
-        for c in range(CHUNKS):
-            e_codes = gather(e_tab, cxt_sb, c * J, J, U32, "e_codes%d" % c)
-            bank = product(w2q, e_codes[:], e_sc[:, c * J : (c + 1) * J], "e_bank%d" % c)
-            seen.append(sigmoid(bank, 1.0, math.log(REST), "seen%d" % c))
 
         click_bank = ps.tile([P, D, P], F32, name="click_bank")
         for d in range(D):
             nc.tensor.transpose(click_bank[:, d, :], click_col[:, d : d + 1].to_broadcast([P, P]), ident[:])
 
+        w1_grp = interleave(w1_raw, "w1_grp")
+        w2_grp = interleave(w2_raw, "w2_grp")
+
+        x_codes = gather(x_tab, offs_sb, 0, S, U32, "x_codes")
+        x_sc = gather(x_stab, offs_sb, 0, S, U8, "x_sc")
+        w1q = quantize(w1_grp, "w1", "w1_scales")
+        miss = sb.tile([P, CHUNKS, D, M_TILES, V], F32, name="miss", tag="w2_raw_then_miss", align_bytes=64)
+        for c in range(CHUNKS):
+            bank = product(w1q, x_codes[:, c * J : (c + 1) * J], x_sc[:, c * J : (c + 1) * J], "x_bank%d" % c)
+            sigmoid(miss[:, c], bank, -1.0, 0.0)
+
+        e_sc = gather(e_stab, cxt_sb, 0, S, U8, "e_sc")
+        w2q = quantize(w2_grp, "w2", "e_stab_then_w2_scales")
+        seen = sb.tile([P, CHUNKS, D, M_TILES, V], F32, name="seen", align_bytes=64)
+        for i in range(S // P):
+            c, v0 = divmod(i * P // D, V)
+            e_codes = gather(e_tab, cxt_sb, i * P, P, U32, "e_codes%d" % i)
+            bank = product(w2q, e_codes[:], e_sc[:, i * P : (i + 1) * P], "e_bank%d" % i)
+            sigmoid(seen[:, c, :, :, v0 : v0 + P // D], bank, 1.0, math.log(REST))
+
         flat = "p d m v -> p (d m v)"
         held = []
         for c in range(CHUNKS):
             both = sb.tile([P, D, M_TILES, V], F32, name="both%d" % c, align_bytes=64)
-            nc.vector.tensor_tensor(both[:].rearrange(flat), miss[c][:].rearrange(flat), seen[c][:].rearrange(flat), ALU.mult)
+            nc.vector.tensor_tensor(both[:].rearrange(flat), miss[:, c].rearrange(flat), seen[:, c].rearrange(flat), ALU.mult)
             lifted = sb.tile([P, D, M_TILES, V], F32, name="lifted%d" % c, align_bytes=64)
             clicks = click_bank[:, :, c * V : (c + 1) * V].unsqueeze(2).broadcast_to([P, D, M_TILES, V])
             nc.vector.tensor_tensor(lifted[:], both[:], clicks, ALU.max)
             held.append(lifted)
 
-        roots = []
-        for c in range(CHUNKS):
-            root = sb.tile([P, D * M_TILES * V], F32, name="root%d" % c, align_bytes=64)
+        half = D * M_TILES * V // 2
+        pieces = [(c, slice(h * half, (h + 1) * half)) for c in range(CHUNKS) for h in range(2)]
+        roots = [sb.tile([P, 2 * half], F32, name="root%d" % c, align_bytes=64) for c in range(CHUNKS)]
+        invs = [sb.tile([P, 2 * half], F32, name="inv%d" % c, align_bytes=64) for c in range(CHUNKS)]
+        for c, cols in pieces:
             nc.scalar.activation(
-                out=root[:], in_=held[c][:].rearrange(flat), func=ACT.Abs_reciprocal_sqrt,
+                out=roots[c][:, cols], in_=held[c][:].rearrange(flat)[:, cols], func=ACT.Abs_reciprocal_sqrt,
                 scale=D * KEEP * KEEP / REST, bias=D * KEEP,
             )
-            roots.append(root)
-
-        half = D * M_TILES * V // 2
+        for c, cols in pieces[:-1]:
+            nc.vector.tensor_tensor(invs[c][:, cols], roots[c][:, cols], roots[c][:, cols], ALU.mult)
+        for c, cols in pieces[-1:]:
+            nc.scalar.activation(out=invs[c][:, cols], in_=roots[c][:, cols], func=ACT.Square)
+        pairs = [sb.tile([P, half], F32, name="pair%d" % c, align_bytes=64) for c in range(CHUNKS)]
         for c in range(CHUNKS):
-            inv = sb.tile([P, 2 * half], F32, name="inv%d" % c, align_bytes=64)
-            if c == 0:
-                nc.vector.tensor_tensor(inv[:], roots[c][:], roots[c][:], ALU.mult)
-            else:
-                nc.scalar.activation(out=inv[:], in_=roots[c][:], func=ACT.Square)
-            pair = sb.tile([P, half], F32, name="pair%d" % c, align_bytes=64)
-            nc.vector.scalar_tensor_tensor(pair[:], inv[:, :half], -1.0, inv[:, half:], ALU.mult, ALU.subtract)
+            nc.vector.scalar_tensor_tensor(pairs[c][:], invs[c][:, :half], -1.0, invs[c][:, half:], ALU.mult, ALU.subtract)
+        for c in range(CHUNKS):
             res = sb.tile([P, M_TILES, V], F32, name="res%d" % c, align_bytes=64)
             nc.vector.scalar_tensor_tensor(
-                res[:].rearrange("p m v -> p (m v)"), pair[:, : half // 2], 1.0 / KEEP, pair[:, half // 2 :], ALU.add, ALU.add
+                res[:].rearrange("p m v -> p (m v)"), pairs[c][:, : half // 2], 1.0 / KEEP, pairs[c][:, half // 2 :], ALU.add, ALU.add
             )
             nc.sync.dma_start(out=out.rearrange("(m p) v -> p m v", p=P)[:, :, c * V : (c + 1) * V], in_=res[:])

@@ -63,8 +63,8 @@ def tile_picked_ytrust_exam_p_kernel(
         warm = sb.tile([P, 2], F32, name="warm", align_bytes=64)
         nc.vector.memset(warm[:, 0:1], 0.0)
         nc.scalar.activation(out=warm[:, 1:2], in_=warm[:, 0:1], func=ACT.Sigmoid)
-        nc.sync.dma_start(offs_sb[:], offs)
         load_words(x_tab, x_words)
+        nc.sync.dma_start(offs_sb[:], offs)
         load_scales(x_stab, x_scales)
         load_weight(w1_raw, w1)
         load_weight(w2_raw, w2)
@@ -76,7 +76,9 @@ def tile_picked_ytrust_exam_p_kernel(
 
         def interleave(raw, name):
             grouped = sb.tile([P, N, PACK], BF16, name=name, align_bytes=64)
-            nc.scalar.copy(out=grouped[:], in_=raw[:].rearrange("p t m -> p m t"))
+            nc.scalar.copy(
+                out=grouped[:].rearrange("p (c i) t -> p c t i", i=4), in_=raw[:].rearrange("p t (c i) -> p c t i", i=4)
+            )
             return grouped
 
         def quantize(grouped, name, tag):
@@ -136,10 +138,12 @@ def tile_picked_ytrust_exam_p_kernel(
             sigmoid(seen[:, c, :, :, v0 : v0 + P // D], bank, 1.0, math.log(REST))
 
         flat = "p d m v -> p (d m v)"
-        held = []
+        held, boths = [], []
         for c in range(CHUNKS):
             both = sb.tile([P, D, M_TILES, V], F32, name="both%d" % c, align_bytes=64)
             nc.vector.tensor_tensor(both[:].rearrange(flat), miss[:, c].rearrange(flat), seen[:, c].rearrange(flat), ALU.mult)
+            boths.append(both)
+        for c, both in enumerate(boths):
             lifted = sb.tile([P, D, M_TILES, V], F32, name="lifted%d" % c, align_bytes=64)
             clicks = click_bank[:, :, c * V : (c + 1) * V].unsqueeze(2).broadcast_to([P, D, M_TILES, V])
             nc.vector.tensor_tensor(lifted[:], both[:], clicks, ALU.max)

import math
from contextlib import ExitStack

import concourse.mybir as mybir
from concourse.masks import make_identity

F32 = mybir.dt.float32
BF16 = mybir.dt.bfloat16
I32 = mybir.dt.int32
U32 = mybir.dt.uint32
U16 = mybir.dt.uint16
U8 = mybir.dt.uint8
FP8X4 = mybir.dt.float8_e4m3fn_x4
ACT = mybir.ActivationFunctionType
ALU = mybir.AluOpType

P = 128
PACK = 4
K, T, S, D, N = 512, 1024, 512, 4, 256
M_TILES = N // P
CHUNKS = 2
J = S // CHUNKS
V = J // D
KEEP = 0.98
REST = 1.0 - KEEP
FLOPS = 2 * 2 * K * N * S


def tile_picked_ytrust_exam_p_kernel(
    tc, x_words, x_scales, e_words, e_scales, w1, w2, click, offs, cxt, out
):
    nc = tc.nc
    with ExitStack() as ctx:
        sb = ctx.enter_context(tc.tile_pool(name="sb", bufs=1))
        ps = ctx.enter_context(tc.psum_pool(name="ps", bufs=1))

        offs_sb = sb.tile([P, S // 16], U16, name="offs_sb")
        cxt_sb = sb.tile([P, S // 16], U16, name="cxt_sb")
        x_tab = sb.tile([P, T], U32, name="x_tab", align_bytes=64)
        e_tab = sb.tile([P, T], U32, name="e_tab", align_bytes=64)
        x_stab = sb.tile([P, T], U8, name="x_stab", align_bytes=64)
        e_stab = sb.tile([P, T], U8, name="e_stab", tag="e_stab_then_w2_scales", align_bytes=64)
        w1_raw = sb.tile([P, PACK, N], F32, name="w1_raw", align_bytes=64)
        w2_raw = sb.tile([P, PACK, N], F32, name="w2_raw", tag="w2_raw_then_miss", align_bytes=64)
        click_col = sb.tile([P, D], F32, name="click_col", align_bytes=64)
        ident = sb.tile([P, P], F32, name="ident", align_bytes=64)

        def load_words(tab, words):
            nc.sync.dma_start(out=tab[:].bitcast(I32), in_=words[0].rearrange("p n t -> p (n t)").bitcast(I32))

        def load_scales(stab, scales):
            for q in range(4):
                nc.sync.dma_start(
                    out=stab[32 * q : 32 * q + 4, :].bitcast(I32),
                    in_=scales[0, 4 * q : 4 * q + 4, :].bitcast(I32),
                )

        def load_weight(raw, w):
            nc.sync.dma_start(out=raw[:], in_=w.rearrange("(p t) m -> p t m", t=PACK))

        nc.vector.memset(x_stab[:].bitcast(I32), 0)
        nc.vector.memset(e_stab[:].bitcast(I32), 0)
        warm = sb.tile([P, 2], F32, name="warm", align_bytes=64)
        nc.vector.memset(warm[:, 0:1], 0.0)
        nc.scalar.activation(out=warm[:, 1:2], in_=warm[:, 0:1], func=ACT.Sigmoid)
        load_words(x_tab, x_words)
        nc.sync.dma_start(offs_sb[:], offs)
        load_scales(x_stab, x_scales)
        load_weight(w1_raw, w1)
        load_weight(w2_raw, w2)
        nc.sync.dma_start(cxt_sb[:], cxt)
        load_scales(e_stab, e_scales)
        load_words(e_tab, e_words)
        nc.gpsimd.dma_start(out=click_col[:], in_=click[0].rearrange("(v d) -> v d", d=D))
        make_identity(nc, ident[:])

        def interleave(raw, name):
            grouped = sb.tile([P, N, PACK], BF16, name=name, align_bytes=64)
            nc.scalar.copy(
                out=grouped[:].rearrange("p (c i) t -> p c t i", i=4), in_=raw[:].rearrange("p t (c i) -> p c t i", i=4)
            )
            return grouped

        def quantize(grouped, name, tag):
            codes = sb.tile([P, N], U32, name=name + "_codes", align_bytes=64)
            scales = sb.tile([P, N], U8, name=name + "_scales", tag=tag, align_bytes=64)
            nc.vector.quantize_mx(
                out=codes[:].bitcast(FP8X4), scales=scales[:], in_=grouped[:].rearrange("p m t -> p (m t)")
            )
            return codes, scales

        def gather(tab, lst, c0, n, dtype, name):
            picked = sb.tile([P, n], dtype, name=name, align_bytes=64)
            nc.vector.tensor_copy(picked[:], tab[:].indirect(lst[:, c0 // 16 : (c0 + n) // 16]))
            return picked

        def product(wq, codes, scales, name):
            bank = ps.tile([P, M_TILES, codes.shape[1]], F32, name=name)
            for m in range(M_TILES):
                nc.tensor.matmul_mx(
                    out=bank[:, m, :],
                    lhsT=wq[0][:, m * P : (m + 1) * P].bitcast(FP8X4),
                    lhsT_scale=wq[1][:, m * P : (m + 1) * P],
                    rhs=codes.bitcast(FP8X4),
                    rhs_scale=scales,
                    start=True,
                    stop=True,
                )
            return bank

        def sigmoid(res, bank, scale, bias):
            nc.scalar.activation(
                out=res, in_=bank[:].rearrange("p m (v d) -> p d m v", d=D), func=ACT.Sigmoid, scale=scale, bias=bias
            )

        click_bank = ps.tile([P, D, P], F32, name="click_bank")
        for d in range(D):
            nc.tensor.transpose(click_bank[:, d, :], click_col[:, d : d + 1].to_broadcast([P, P]), ident[:])

        w1_grp = interleave(w1_raw, "w1_grp")
        w2_grp = interleave(w2_raw, "w2_grp")

        x_codes = gather(x_tab, offs_sb, 0, S, U32, "x_codes")
        x_sc = gather(x_stab, offs_sb, 0, S, U8, "x_sc")
        w1q = quantize(w1_grp, "w1", "w1_scales")
        miss = sb.tile([P, CHUNKS, D, M_TILES, V], F32, name="miss", tag="w2_raw_then_miss", align_bytes=64)
        for c in range(CHUNKS):
            bank = product(w1q, x_codes[:, c * J : (c + 1) * J], x_sc[:, c * J : (c + 1) * J], "x_bank%d" % c)
            sigmoid(miss[:, c], bank, -1.0, 0.0)

        e_sc = gather(e_stab, cxt_sb, 0, S, U8, "e_sc")
        w2q = quantize(w2_grp, "w2", "e_stab_then_w2_scales")
        seen = sb.tile([P, CHUNKS, D, M_TILES, V], F32, name="seen", align_bytes=64)
        for i in range(S // P):
            c, v0 = divmod(i * P // D, V)
            e_codes = gather(e_tab, cxt_sb, i * P, P, U32, "e_codes%d" % i)
            bank = product(w2q, e_codes[:], e_sc[:, i * P : (i + 1) * P], "e_bank%d" % i)
            sigmoid(seen[:, c, :, :, v0 : v0 + P // D], bank, 1.0, math.log(REST))

        flat = "p d m v -> p (d m v)"
        held, boths = [], []
        for c in range(CHUNKS):
            both = sb.tile([P, D, M_TILES, V], F32, name="both%d" % c, align_bytes=64)
            nc.vector.tensor_tensor(both[:].rearrange(flat), miss[:, c].rearrange(flat), seen[:, c].rearrange(flat), ALU.mult)
            boths.append(both)
        for c, both in enumerate(boths):
            lifted = sb.tile([P, D, M_TILES, V], F32, name="lifted%d" % c, align_bytes=64)
            clicks = click_bank[:, :, c * V : (c + 1) * V].unsqueeze(2).broadcast_to([P, D, M_TILES, V])
            nc.vector.tensor_tensor(lifted[:], both[:], clicks, ALU.max)
            held.append(lifted)

        half = D * M_TILES * V // 2
        pieces = [(c, slice(h * half, (h + 1) * half)) for c in range(CHUNKS) for h in range(2)]
        roots = [sb.tile([P, 2 * half], F32, name="root%d" % c, align_bytes=64) for c in range(CHUNKS)]
        invs = [sb.tile([P, 2 * half], F32, name="inv%d" % c, align_bytes=64) for c in range(CHUNKS)]
        for c, cols in pieces:
            nc.scalar.activation(
                out=roots[c][:, cols], in_=held[c][:].rearrange(flat)[:, cols], func=ACT.Abs_reciprocal_sqrt,
                scale=D * KEEP * KEEP / REST, bias=D * KEEP,
            )
        for c, cols in pieces[:-1]:
            nc.vector.tensor_tensor(invs[c][:, cols], roots[c][:, cols], roots[c][:, cols], ALU.mult)
        for c, cols in pieces[-1:]:
            nc.scalar.activation(out=invs[c][:, cols], in_=roots[c][:, cols], func=ACT.Square)
        pairs = [sb.tile([P, half], F32, name="pair%d" % c, align_bytes=64) for c in range(CHUNKS)]
        for c in range(CHUNKS):
            nc.vector.scalar_tensor_tensor(pairs[c][:], invs[c][:, :half], -1.0, invs[c][:, half:], ALU.mult, ALU.subtract)
        for c in range(CHUNKS):
            res = sb.tile([P, M_TILES, V], F32, name="res%d" % c, align_bytes=64)
            nc.vector.scalar_tensor_tensor(
                res[:].rearrange("p m v -> p (m v)"), pairs[c][:, : half // 2], 1.0 / KEEP, pairs[c][:, half // 2 :], ALU.add, ALU.add
            )
            nc.sync.dma_start(out=out.rearrange("(m p) v -> p m v", p=P)[:, :, c * V : (c + 1) * V], in_=res[:])
